import numpy as np, ml_dtypes
CORES = [22,46,70,150,174,198,278,302,326,406,430,454]
N = 12
DEG, TK = 4, 128
MASK = [[3,4,10,0],[3,4,10,1],[3,4,10,2],[3,4,10,0],[3,4,10,0],[3,4,10,5],[3,4,10,6],[3,4,10,7],[3,4,10,8],[3,4,10,9],[3,4,10,0],[3,4,10,11]]
def setup_inputs(rng):
    return {"x": rng.standard_normal((N, 128, TK), dtype=np.float32).astype(ml_dtypes.bfloat16), "w": rng.standard_normal((N, 128, DEG * 128), dtype=np.float32).astype(ml_dtypes.bfloat16)}
def setup_inputs_big(rng):
    d = setup_inputs(rng)
    for k in ("x", "w"): d[k] = (d[k].astype(np.float32) * 1024.0).astype(d[k].dtype)
    return d
def setup_inputs_small(rng):
    d = setup_inputs(rng)
    for k in ("x", "w"): d[k] = (d[k].astype(np.float32) * (1 / 1024.0)).astype(d[k].dtype)
    return d
def setup_inputs_apart(rng):
    d = setup_inputs(rng)
    f = (10.0 ** rng.permutation(np.linspace(-1.5, 1.5, N))).astype(np.float32).reshape(N, 1, 1)
    for k in ("x", "w"): d[k] = (d[k].astype(np.float32) * f).astype(d[k].dtype)
    return d
def reference(x, w):
    X, W = x.astype(np.float64), w.astype(np.float64)
    y = np.zeros((N, 128, TK))
    for r in range(N):
        for i, j in enumerate(MASK[r]):
            y[r] += W[r][:, 128 * i:128 * i + 128].T @ X[j]
    return {"y": y.astype(ml_dtypes.bfloat16 if x.dtype != np.float64 else np.float64)}

@@ -1,0 +1,146 @@
+from concourse.bass import DstId, RemoteDMATransfer
+
+WORLD = 512
+TK = 128
+MOVERS = 4
+
+SCRATCH = {
+    "xd": ("dram", [MOVERS, TK, TK], "bfloat16"),
+    "xs": ("sbuf", [TK, 4 * TK], "bfloat16"),
+    "ws": ("sbuf", [TK, 4 * TK], "bfloat16"),
+    "ys": ("sbuf", [TK, TK], "bfloat16"),
+    "acc": ("psum", [TK, TK], "float32"),
+}
+SEMAPHORES = (["ldd", "ldx", "ldw", "sent", "mm", "cp", "st"]
+              + ["a%d" % k for k in range(MOVERS)]
+              + ["u%d" % k for k in range(MOVERS)])
+
+
+def _count(mask):
+    return bin(mask).count("1")
+
+
+def _route(T, topo):
+    cores = list(T.cores)
+    need = T.tables["MASK"]
+    n = len(cores)
+    users = [[r for r in range(n) if r != j and j in need[r]] for j in range(n)]
+    movers = [j for j in range(n) if users[j]]
+    near = {j: [r for r in users[j] if topo.may_write(cores[j], cores[r])] for j in movers}
+    far = [(j, r) for j in movers for r in users[j] if r not in near[j]]
+    late = set(r for _, r in far)
+
+    wish = {}
+    for j, r in far:
+        mid = [m for m in near[j]
+               if topo.may_write(cores[m], cores[r]) and topo.chip(cores[m]) == topo.chip(cores[r])
+               and topo.rack(topo.host(cores[m])) == topo.rack(topo.host(cores[j]))]
+        wish.setdefault(mid[0], []).append((j, r))
+    taken = set(cores)
+    via = {}
+    for m in sorted(wish):
+        cm = cores[m]
+        pairs = sorted(wish[m], key=lambda p: topo.same_plane(cores[p[0]], cm))
+        via[pairs[0]] = cm
+        for j, r in pairs[1:]:
+            spare = [c for c in range(WORLD)
+                     if c not in taken and topo.host(c) == topo.host(cm) and topo.chip(c) == topo.chip(cm)
+                     and topo.die(c) == topo.die(cores[j])
+                     and topo.may_write(cores[j], c) and topo.may_write(c, cores[r])]
+            via[(j, r)] = spare[0]
+            taken.add(spare[0])
+
+    jobs, lands = {}, {}
+    for k, j in enumerate(movers):
+        src = cores[j]
+        first = [via[p] for p in far if p[0] == j]
+        rest = [cores[r] for r in sorted(near[j], key=lambda r: r in late) if cores[r] not in first]
+        place = 0
+        for call in (first, rest):
+            if not call:
+                continue
+            mask = topo.mask(src, call[0])
+            for c in call:
+                mask &= topo.mask(src, c)
+            jobs.setdefault(src, []).append(("ldd", 16, k, mask, [(c, "dram", k) for c in call]))
+            for c in call:
+                lands[(c, k)] = (1, place, "dram", _count(mask))
+                place += 1
+    for k, j in enumerate(movers):
+        for p in far:
+            if p[0] != j:
+                continue
+            c, dst = via[p], cores[p[1]]
+            mask = topo.mask(c, dst)
+            jobs.setdefault(c, []).append(("a%d" % k, lands[(c, k)][3], k, mask, [(dst, "sbuf", need[p[1]].index(j))]))
+            lands[(dst, k)] = (2, 0, "sbuf", _count(mask))
+    return movers, jobs, lands
+
+
+def rank_program(g, core, T, topo):
+    movers, jobs, lands = _route(T, topo)
+    rank = T.rank_of(core)
+    sem = T.sem
+
+    def block(i):
+        return T.xs[:, i * TK:(i + 1) * TK]
+
+    order = []
+    if rank is not None:
+        need = T.tables["MASK"][rank]
+        owner = rank in movers
+        if owner:
+            g.sync.dma_start(T.xd[movers.index(rank)], T.x[:]).then_inc(sem.ldd, 16)
+        if rank in need:
+            g.sync.dma_start(block(need.index(rank)), T.x[:]).then_inc(sem.ldx, 16)
+        (g.sync if owner else g.scalar).dma_start(T.ws[:], T.w[:]).then_inc(sem.ldw, 16)
+        for i, j in enumerate(need):
+            if j == rank:
+                order.append(((0, 0), i, None))
+            else:
+                k = movers.index(j)
+                order.append((lands[(core, k)][:2], i, k))
+        order.sort()
+        turn = 0
+        for _, i, k in order:
+            if k is not None and lands[(core, k)][2] == "dram":
+                q = (g.scalar, g.sync)[turn % 2]
+                turn += 1
+                q.wait_ge(sem["a%d" % k], lands[(core, k)][3])
+                q.dma_start(block(i), T.xd[k]).then_inc(sem["u%d" % k], 16)
+
+    sent = 0
+    seen = None
+    for wait, count, k, mask, dsts in jobs.get(core, []):
+        if wait != seen:
+            g.wait_ge(sem[wait], count)
+            seen = wait
+        ids, aps = [], []
+        for c, where, i in dsts:
+            rid, pid = topo.addr(c, core)
+            ids.append(DstId(rid=rid, pnc=pid))
+            aps.append(T.xd[i] if where == "dram" else block(i))
+        g.remote_dma_fused([RemoteDMATransfer(dst_ids=ids, dma_engine_mask=mask, remote_sem=sem["a%d" % k],
+                                              srcs=[T.xd[k]], dsts=aps)], local_sem=sem.sent)
+        sent += _count(mask)
+    if sent:
+        g.wait_ge(sem.sent, sent)
+
+    if rank is None:
+        return
+    g.tensor.wait_ge(sem.ldw, 16)
+    last = None
+    for pos, (_, i, k) in enumerate(order):
+        if k is None:
+            g.tensor.wait_ge(sem.ldx, 16)
+        elif lands[(core, k)][2] == "dram":
+            g.tensor.wait_ge(sem["u%d" % k], 16)
+        else:
+            g.tensor.wait_ge(sem["a%d" % k], lands[(core, k)][3])
+        last = g.tensor.matmul(T.acc[:], T.ws[:, i * TK:(i + 1) * TK], block(i), pos == 0, pos == len(order) - 1)
+    last.then_inc(sem.mm, 1)
+    g.vector.wait_ge(sem.mm, 1)
+    g.vector.tensor_copy(T.ys[:], T.acc[:]).then_inc(sem.cp, 1)
+    g.sync.wait_ge(sem.cp, 1)
+    g.sync.dma_start(T.y[:], T.ys[:]).then_inc(sem.st, 16)
+    g.sync.wait_ge(sem.st, 16)

@@ -12,12 +12,16 @@ SCRATCH = {
     "acc": ("psum", [TK, TK], "float32"),
 }
 SEMAPHORES = (["ldd", "ldx", "ldw", "sent", "mm", "cp", "st"]
-              + ["a%d" % k for k in range(MOVERS)]
-              + ["u%d" % k for k in range(MOVERS)])
+              + ["a%d" % k for k in range(MOVERS)])
 
 
 def _count(mask):
     return bin(mask).count("1")
+
+
+def _turn(seq, k):
+    k = k % len(seq) if seq else 0
+    return seq[k:] + seq[:k]
 
 
 def _route(T, topo):
@@ -50,30 +54,38 @@ def _route(T, topo):
             via[(j, r)] = spare[0]
             taken.add(spare[0])
 
+    def spot(c, j, k):
+        if c in cores:
+            return (c, ("sbuf", need[cores.index(c)].index(j)))
+        return (c, ("dram", k))
+
     jobs, lands = {}, {}
     for k, j in enumerate(movers):
         src = cores[j]
         first = [via[p] for p in far if p[0] == j]
-        rest = [cores[r] for r in sorted(near[j], key=lambda r: r in late) if cores[r] not in first]
-        place = 0
-        for call in (first, rest):
+        calls = [[spot(c, j, k) for c in first],
+                 [spot(cores[r], j, k) for r in near[j] if r not in late and cores[r] not in first],
+                 [spot(cores[r], j, k) for r in near[j] if r in late and cores[r] not in first]]
+        turn = 0
+        for call in calls:
             if not call:
                 continue
-            mask = topo.mask(src, call[0])
-            for c in call:
+            call = _turn(call, k)
+            mask = topo.mask(src, call[0][0])
+            for c, _ in call:
                 mask &= topo.mask(src, c)
-            jobs.setdefault(src, []).append(("ldd", 16, k, mask, [(c, "dram", k) for c in call]))
-            for c in call:
-                lands[(c, k)] = (1, place, "dram", _count(mask))
-                place += 1
+            jobs.setdefault(src, []).append(("ldd", 16, k, mask, ("dram", k), call))
+            for c, place in call:
+                lands[(c, k)] = (1, turn, _count(mask), place)
+                turn += 1
     for k, j in enumerate(movers):
         for p in far:
             if p[0] != j:
                 continue
             c, dst = via[p], cores[p[1]]
             mask = topo.mask(c, dst)
-            jobs.setdefault(c, []).append(("a%d" % k, lands[(c, k)][3], k, mask, [(dst, "sbuf", need[p[1]].index(j))]))
-            lands[(dst, k)] = (2, 0, "sbuf", _count(mask))
+            jobs.setdefault(c, []).append(("a%d" % k, lands[(c, k)][2], k, mask, lands[(c, k)][3], [spot(dst, j, k)]))
+            lands[(dst, k)] = (2, 0, _count(mask), None)
     return movers, jobs, lands
 
 
@@ -82,8 +94,10 @@ def rank_program(g, core, T, topo):
     rank = T.rank_of(core)
     sem = T.sem
 
-    def block(i):
-        return T.xs[:, i * TK:(i + 1) * TK]
+    def at(place):
+        if place[0] == "dram":
+            return T.xd[place[1]]
+        return T.xs[:, place[1] * TK:(place[1] + 1) * TK]
 
     order = []
     if rank is not None:
@@ -92,7 +106,7 @@ def rank_program(g, core, T, topo):
         if owner:
             g.sync.dma_start(T.xd[movers.index(rank)], T.x[:]).then_inc(sem.ldd, 16)
         if rank in need:
-            g.sync.dma_start(block(need.index(rank)), T.x[:]).then_inc(sem.ldx, 16)
+            g.sync.dma_start(at(("sbuf", need.index(rank))), T.x[:]).then_inc(sem.ldx, 16)
         (g.sync if owner else g.scalar).dma_start(T.ws[:], T.w[:]).then_inc(sem.ldw, 16)
         for i, j in enumerate(need):
             if j == rank:
@@ -101,27 +115,20 @@ def rank_program(g, core, T, topo):
                 k = movers.index(j)
                 order.append((lands[(core, k)][:2], i, k))
         order.sort()
-        turn = 0
-        for _, i, k in order:
-            if k is not None and lands[(core, k)][2] == "dram":
-                q = (g.scalar, g.sync)[turn % 2]
-                turn += 1
-                q.wait_ge(sem["a%d" % k], lands[(core, k)][3])
-                q.dma_start(block(i), T.xd[k]).then_inc(sem["u%d" % k], 16)
 
     sent = 0
     seen = None
-    for wait, count, k, mask, dsts in jobs.get(core, []):
+    for wait, count, k, mask, src, dsts in jobs.get(core, []):
         if wait != seen:
             g.wait_ge(sem[wait], count)
             seen = wait
         ids, aps = [], []
-        for c, where, i in dsts:
+        for c, place in dsts:
             rid, pid = topo.addr(c, core)
             ids.append(DstId(rid=rid, pnc=pid))
-            aps.append(T.xd[i] if where == "dram" else block(i))
+            aps.append(at(place))
         g.remote_dma_fused([RemoteDMATransfer(dst_ids=ids, dma_engine_mask=mask, remote_sem=sem["a%d" % k],
-                                              srcs=[T.xd[k]], dsts=aps)], local_sem=sem.sent)
+                                              srcs=[at(src)], dsts=aps)], local_sem=sem.sent)
         sent += _count(mask)
     if sent:
         g.wait_ge(sem.sent, sent)
@@ -133,11 +140,9 @@ def rank_program(g, core, T, topo):
     for pos, (_, i, k) in enumerate(order):
         if k is None:
             g.tensor.wait_ge(sem.ldx, 16)
-        elif lands[(core, k)][2] == "dram":
-            g.tensor.wait_ge(sem["u%d" % k], 16)
         else:
-            g.tensor.wait_ge(sem["a%d" % k], lands[(core, k)][3])
-        last = g.tensor.matmul(T.acc[:], T.ws[:, i * TK:(i + 1) * TK], block(i), pos == 0, pos == len(order) - 1)
+            g.tensor.wait_ge(sem["a%d" % k], lands[(core, k)][2])
+        last = g.tensor.matmul(T.acc[:], T.ws[:, i * TK:(i + 1) * TK], at(("sbuf", i)), pos == 0, pos == len(order) - 1)
     last.then_inc(sem.mm, 1)
     g.vector.wait_ge(sem.mm, 1)
     g.vector.tensor_copy(T.ys[:], T.acc[:]).then_inc(sem.cp, 1)

@@ -1,11 +1,10 @@
 from concourse.bass import DstId, RemoteDMATransfer
 
-WORLD = 512
 TK = 128
 MOVERS = 4
 
 SCRATCH = {
-    "xd": ("dram", [MOVERS, TK, TK], "bfloat16"),
+    "xd": ("dram", [TK, TK], "bfloat16"),
     "xs": ("sbuf", [TK, 4 * TK], "bfloat16"),
     "ws": ("sbuf", [TK, 4 * TK], "bfloat16"),
     "ys": ("sbuf", [TK, TK], "bfloat16"),
@@ -19,6 +18,11 @@ def _count(mask):
     return bin(mask).count("1")
 
 
+def _halves(mask):
+    bits = [b for b in range(16) if mask >> b & 1]
+    return sum(1 << b for b in bits[0::2]), sum(1 << b for b in bits[1::2])
+
+
 def _turn(seq, k):
     k = k % len(seq) if seq else 0
     return seq[k:] + seq[:k]
@@ -30,119 +34,128 @@ def _route(T, topo):
     n = len(cores)
     users = [[r for r in range(n) if r != j and j in need[r]] for j in range(n)]
     movers = [j for j in range(n) if users[j]]
-    near = {j: [r for r in users[j] if topo.may_write(cores[j], cores[r])] for j in movers}
-    far = [(j, r) for j in movers for r in users[j] if r not in near[j]]
-    late = set(r for _, r in far)
 
-    wish = {}
-    for j, r in far:
-        mid = [m for m in near[j]
-               if topo.may_write(cores[m], cores[r]) and topo.chip(cores[m]) == topo.chip(cores[r])
-               and topo.rack(topo.host(cores[m])) == topo.rack(topo.host(cores[j]))]
-        wish.setdefault(mid[0], []).append((j, r))
-    taken = set(cores)
-    via = {}
-    for m in sorted(wish):
-        cm = cores[m]
-        pairs = sorted(wish[m], key=lambda p: topo.same_plane(cores[p[0]], cm))
-        via[pairs[0]] = cm
-        for j, r in pairs[1:]:
-            spare = [c for c in range(WORLD)
-                     if c not in taken and topo.host(c) == topo.host(cm) and topo.chip(c) == topo.chip(cm)
-                     and topo.die(c) == topo.die(cores[j])
-                     and topo.may_write(cores[j], c) and topo.may_write(c, cores[r])]
-            via[(j, r)] = spare[0]
-            taken.add(spare[0])
+    def rack(r):
+        return topo.rack(topo.host(cores[r]))
 
-    def spot(c, j, k):
-        if c in cores:
-            return (c, ("sbuf", need[cores.index(c)].index(j)))
-        return (c, ("dram", k))
+    def ok(a, b):
+        return topo.may_write(cores[a], cores[b])
+
+    def same_number(a, b):
+        return topo.chip(cores[a]) == topo.chip(cores[b])
+
+    def engines(s, dsts):
+        mask = topo.mask(cores[s], cores[dsts[0]])
+        for r in dsts:
+            mask &= topo.mask(cores[s], cores[r])
+        return mask
+
+    near = {j: [r for r in users[j] if ok(j, r)] for j in movers}
+    far = {j: [r for r in users[j] if not ok(j, r)] for j in movers}
+    late = set(r for j in movers for r in far[j])
+    home = {j: [r for r in near[j] if rack(r) == rack(j)] for j in movers}
+    away = {j: [r for r in near[j] if rack(r) != rack(j)] for j in movers}
+    head = {}
+    for j in movers:
+        if far[j]:
+            head[j] = [r for r in away[j] if same_number(r, j) and all(ok(r, u) for u in far[j])][0]
+    busy = set(head.values())
+    side = {}
+    for j in movers:
+        if far[j]:
+            side[j] = [(m, u) for m in home[j] for u in far[j] if m not in busy and ok(m, u) and same_number(m, u)][0]
+            busy.add(side[j][0])
 
     jobs, lands = {}, {}
     for k, j in enumerate(movers):
-        src = cores[j]
-        first = [via[p] for p in far if p[0] == j]
-        calls = [[spot(c, j, k) for c in first],
-                 [spot(cores[r], j, k) for r in near[j] if r not in late and cores[r] not in first],
-                 [spot(cores[r], j, k) for r in near[j] if r in late and cores[r] not in first]]
-        turn = 0
-        for call in calls:
-            if not call:
-                continue
-            call = _turn(call, k)
-            mask = topo.mask(src, call[0][0])
-            for c, _ in call:
-                mask &= topo.mask(src, c)
-            jobs.setdefault(src, []).append(("ldd", 16, k, mask, ("dram", k), call))
-            for c, place in call:
-                lands[(c, k)] = (1, turn, _count(mask), place)
-                turn += 1
+        first = [side[j][0]] if j in side else []
+        rest = [r for r in home[j] if r not in first]
+        inrack = first + [r for r in rest if r not in late] + _turn([r for r in rest if r in late], k)
+        cable = ([head[j]] if j in head else []) + _turn([r for r in away[j] if r != head.get(j)], k)
+        while len(inrack) > len(cable) + 1:
+            cable.append(inrack.pop())
+        ma, mb = _halves(engines(j, inrack + cable))
+        jobs.setdefault(cores[j], []).append((k, True, [(ma, inrack), (mb, cable)]))
+        for t, r in enumerate(inrack):
+            lands[(r, k)] = (1.0 + t, _count(ma))
+        for t, r in enumerate(cable):
+            lands[(r, k)] = (2.5 + 2.5 * t, _count(mb))
     for k, j in enumerate(movers):
-        for p in far:
-            if p[0] != j:
-                continue
-            c, dst = via[p], cores[p[1]]
-            mask = topo.mask(c, dst)
-            jobs.setdefault(c, []).append(("a%d" % k, lands[(c, k)][2], k, mask, lands[(c, k)][3], [spot(dst, j, k)]))
-            lands[(dst, k)] = (2, 0, _count(mask), None)
+        if j not in head:
+            continue
+        m, u = side[j]
+        mask = _halves(engines(m, [u]))[1]
+        jobs.setdefault(cores[m], []).append((k, False, [(mask, [u])]))
+        lands[(u, k)] = (20.0, _count(mask))
+        rest = [r for r in far[j] if r != u]
+        mask = engines(head[j], rest)
+        jobs.setdefault(cores[head[j]], []).append((k, False, [(mask, rest)]))
+        for t, r in enumerate(rest):
+            lands[(r, k)] = (20.0 + t, _count(mask))
     return movers, jobs, lands
 
 
 def rank_program(g, core, T, topo):
-    movers, jobs, lands = _route(T, topo)
     rank = T.rank_of(core)
+    if rank is None:
+        return
+    movers, jobs, lands = _route(T, topo)
+    cores = list(T.cores)
+    table = T.tables["MASK"]
+    need = table[rank]
     sem = T.sem
 
-    def at(place):
-        if place[0] == "dram":
-            return T.xd[place[1]]
-        return T.xs[:, place[1] * TK:(place[1] + 1) * TK]
+    def block(r, j):
+        i = table[r].index(j)
+        return T.xs[:, i * TK:(i + 1) * TK]
 
-    order = []
-    if rank is not None:
-        need = T.tables["MASK"][rank]
-        owner = rank in movers
-        if owner:
-            g.sync.dma_start(T.xd[movers.index(rank)], T.x[:]).then_inc(sem.ldd, 16)
-        if rank in need:
-            g.sync.dma_start(at(("sbuf", need.index(rank))), T.x[:]).then_inc(sem.ldx, 16)
-        (g.sync if owner else g.scalar).dma_start(T.ws[:], T.w[:]).then_inc(sem.ldw, 16)
-        for i, j in enumerate(need):
-            if j == rank:
-                order.append(((0, 0), i, None))
-            else:
-                k = movers.index(j)
-                order.append((lands[(core, k)][:2], i, k))
-        order.sort()
+    owner = rank in movers
+    if owner:
+        g.sync.dma_start(T.xd[:], T.x[:]).then_inc(sem.ldd, 16)
+    if rank in need:
+        g.sync.dma_start(block(rank, rank), T.x[:]).then_inc(sem.ldx, 16)
+    (g.sync if owner else g.scalar).dma_start(T.ws[:], T.w[:]).then_inc(sem.ldw, 16)
 
     sent = 0
-    seen = None
-    for wait, count, k, mask, src, dsts in jobs.get(core, []):
-        if wait != seen:
-            g.wait_ge(sem[wait], count)
-            seen = wait
-        ids, aps = [], []
-        for c, place in dsts:
-            rid, pid = topo.addr(c, core)
-            ids.append(DstId(rid=rid, pnc=pid))
-            aps.append(at(place))
-        g.remote_dma_fused([RemoteDMATransfer(dst_ids=ids, dma_engine_mask=mask, remote_sem=sem["a%d" % k],
-                                              srcs=[at(src)], dsts=aps)], local_sem=sem.sent)
-        sent += _count(mask)
+    for k, own, streams in jobs.get(core, []):
+        if own:
+            g.wait_ge(sem.ldd, 16)
+        else:
+            g.wait_ge(sem["a%d" % k], lands[(rank, k)][1])
+        j = movers[k]
+        transfers = []
+        for mask, dsts in streams:
+            if not dsts:
+                continue
+            ids = []
+            for r in dsts:
+                rid, pid = topo.addr(cores[r], core)
+                ids.append(DstId(rid=rid, pnc=pid))
+            transfers.append(RemoteDMATransfer(dst_ids=ids, dma_engine_mask=mask, remote_sem=sem["a%d" % k],
+                                               srcs=[T.xd[:] if own else block(rank, j)],
+                                               dsts=[block(r, j) for r in dsts]))
+            sent += _count(mask)
+        g.remote_dma_fused(transfers, local_sem=sem.sent)
     if sent:
         g.wait_ge(sem.sent, sent)
 
-    if rank is None:
-        return
+    order = []
+    for i, j in enumerate(need):
+        if j == rank:
+            order.append((0.0, i, None))
+        else:
+            k = movers.index(j)
+            order.append((lands[(rank, k)][0], i, k))
+    order.sort()
     g.tensor.wait_ge(sem.ldw, 16)
     last = None
     for pos, (_, i, k) in enumerate(order):
         if k is None:
             g.tensor.wait_ge(sem.ldx, 16)
         else:
-            g.tensor.wait_ge(sem["a%d" % k], lands[(core, k)][2])
-        last = g.tensor.matmul(T.acc[:], T.ws[:, i * TK:(i + 1) * TK], at(("sbuf", i)), pos == 0, pos == len(order) - 1)
+            g.tensor.wait_ge(sem["a%d" % k], lands[(rank, k)][1])
+        last = g.tensor.matmul(T.acc[:], T.ws[:, i * TK:(i + 1) * TK], T.xs[:, i * TK:(i + 1) * TK],
+                               pos == 0, pos == len(order) - 1)
     last.then_inc(sem.mm, 1)
     g.vector.wait_ge(sem.mm, 1)
     g.vector.tensor_copy(T.ys[:], T.acc[:]).then_inc(sem.cp, 1)

from concourse.bass import DstId, RemoteDMATransfer

TK = 128
MOVERS = 4

SCRATCH = {
    "xd": ("dram", [TK, TK], "bfloat16"),
    "xs": ("sbuf", [TK, 4 * TK], "bfloat16"),
    "ws": ("sbuf", [TK, 4 * TK], "bfloat16"),
    "ys": ("sbuf", [TK, TK], "bfloat16"),
    "acc": ("psum", [TK, TK], "float32"),
}
SEMAPHORES = (["ldd", "ldx", "ldw", "sent", "mm", "cp", "st"]
              + ["a%d" % k for k in range(MOVERS)])


def _count(mask):
    return bin(mask).count("1")


def _halves(mask):
    bits = [b for b in range(16) if mask >> b & 1]
    return sum(1 << b for b in bits[0::2]), sum(1 << b for b in bits[1::2])


def _turn(seq, k):
    k = k % len(seq) if seq else 0
    return seq[k:] + seq[:k]


def _route(T, topo):
    cores = list(T.cores)
    need = T.tables["MASK"]
    n = len(cores)
    users = [[r for r in range(n) if r != j and j in need[r]] for j in range(n)]
    movers = [j for j in range(n) if users[j]]

    def rack(r):
        return topo.rack(topo.host(cores[r]))

    def ok(a, b):
        return topo.may_write(cores[a], cores[b])

    def same_number(a, b):
        return topo.chip(cores[a]) == topo.chip(cores[b])

    def engines(s, dsts):
        mask = topo.mask(cores[s], cores[dsts[0]])
        for r in dsts:
            mask &= topo.mask(cores[s], cores[r])
        return mask

    near = {j: [r for r in users[j] if ok(j, r)] for j in movers}
    far = {j: [r for r in users[j] if not ok(j, r)] for j in movers}
    late = set(r for j in movers for r in far[j])
    home = {j: [r for r in near[j] if rack(r) == rack(j)] for j in movers}
    away = {j: [r for r in near[j] if rack(r) != rack(j)] for j in movers}
    head = {}
    for j in movers:
        if far[j]:
            head[j] = [r for r in away[j] if same_number(r, j) and all(ok(r, u) for u in far[j])][0]
    busy = set(head.values())
    side = {}
    for j in movers:
        if far[j]:
            side[j] = [(m, u) for m in home[j] for u in far[j] if m not in busy and ok(m, u) and same_number(m, u)][0]
            busy.add(side[j][0])

    jobs, lands = {}, {}
    for k, j in enumerate(movers):
        first = [side[j][0]] if j in side else []
        rest = [r for r in home[j] if r not in first]
        inrack = first + [r for r in rest if r not in late] + _turn([r for r in rest if r in late], k)
        cable = ([head[j]] if j in head else []) + _turn([r for r in away[j] if r != head.get(j)], k)
        while len(inrack) > len(cable) + 1:
            cable.append(inrack.pop())
        ma, mb = _halves(engines(j, inrack + cable))
        jobs.setdefault(cores[j], []).append((k, True, [(ma, inrack), (mb, cable)]))
        for t, r in enumerate(inrack):
            lands[(r, k)] = (1.0 + t, _count(ma))
        for t, r in enumerate(cable):
            lands[(r, k)] = (2.5 + 2.5 * t, _count(mb))
    for k, j in enumerate(movers):
        if j not in head:
            continue
        m, u = side[j]
        mask = _halves(engines(m, [u]))[1]
        jobs.setdefault(cores[m], []).append((k, False, [(mask, [u])]))
        lands[(u, k)] = (20.0, _count(mask))
        rest = [r for r in far[j] if r != u]
        mask = engines(head[j], rest)
        jobs.setdefault(cores[head[j]], []).append((k, False, [(mask, rest)]))
        for t, r in enumerate(rest):
            lands[(r, k)] = (20.0 + t, _count(mask))
    return movers, jobs, lands


def rank_program(g, core, T, topo):
    rank = T.rank_of(core)
    if rank is None:
        return
    movers, jobs, lands = _route(T, topo)
    cores = list(T.cores)
    table = T.tables["MASK"]
    need = table[rank]
    sem = T.sem

    def block(r, j):
        i = table[r].index(j)
        return T.xs[:, i * TK:(i + 1) * TK]

    owner = rank in movers
    if owner:
        g.sync.dma_start(T.xd[:], T.x[:]).then_inc(sem.ldd, 16)
    if rank in need:
        g.sync.dma_start(block(rank, rank), T.x[:]).then_inc(sem.ldx, 16)
    (g.sync if owner else g.scalar).dma_start(T.ws[:], T.w[:]).then_inc(sem.ldw, 16)

    sent = 0
    for k, own, streams in jobs.get(core, []):
        if own:
            g.wait_ge(sem.ldd, 16)
        else:
            g.wait_ge(sem["a%d" % k], lands[(rank, k)][1])
        j = movers[k]
        transfers = []
        for mask, dsts in streams:
            if not dsts:
                continue
            ids = []
            for r in dsts:
                rid, pid = topo.addr(cores[r], core)
                ids.append(DstId(rid=rid, pnc=pid))
            transfers.append(RemoteDMATransfer(dst_ids=ids, dma_engine_mask=mask, remote_sem=sem["a%d" % k],
                                               srcs=[T.xd[:] if own else block(rank, j)],
                                               dsts=[block(r, j) for r in dsts]))
            sent += _count(mask)
        g.remote_dma_fused(transfers, local_sem=sem.sent)
    if sent:
        g.wait_ge(sem.sent, sent)

    order = []
    for i, j in enumerate(need):
        if j == rank:
            order.append((0.0, i, None))
        else:
            k = movers.index(j)
            order.append((lands[(rank, k)][0], i, k))
    order.sort()
    g.tensor.wait_ge(sem.ldw, 16)
    last = None
    for pos, (_, i, k) in enumerate(order):
        if k is None:
            g.tensor.wait_ge(sem.ldx, 16)
        else:
            g.tensor.wait_ge(sem["a%d" % k], lands[(rank, k)][1])
        last = g.tensor.matmul(T.acc[:], T.ws[:, i * TK:(i + 1) * TK], T.xs[:, i * TK:(i + 1) * TK],
                               pos == 0, pos == len(order) - 1)
    last.then_inc(sem.mm, 1)
    g.vector.wait_ge(sem.mm, 1)
    g.vector.tensor_copy(T.ys[:], T.acc[:]).then_inc(sem.cp, 1)
    g.sync.wait_ge(sem.cp, 1)
    g.sync.dma_start(T.y[:], T.ys[:]).then_inc(sem.st, 16)
    g.sync.wait_ge(sem.st, 16)
